import numpy as np
import ml_dtypes


def mxq(x, axis, fmt="e4m3"):
    dtype, down = {"e4m3": (ml_dtypes.float8_e4m3fn, 7), "e5m2": (ml_dtypes.float8_e5m2, 14)}[fmt]
    v = np.moveaxis(np.asarray(x, np.float32).astype(ml_dtypes.bfloat16).astype(np.float64), axis, -1)
    blocks = v.reshape(v.shape[:-1] + (-1, 32))
    amax = np.abs(blocks).max(-1, keepdims=True)
    byte = np.maximum(np.where(amax > 0, np.frexp(amax)[1] - 1 + 127, 0) - down, 1)
    scale = np.exp2(byte - 127.0)
    codes = (blocks / scale).astype(np.float32).astype(dtype).astype(np.float64)
    return np.moveaxis((codes * scale).reshape(v.shape), -1, axis)


WIDE = False


def mx_kscale(k):
    if not WIDE:
        return np.ones(k)
    levels = np.array([10, -10, 5, -5, 0])
    if k % 512:
        return np.exp2(np.random.permutation(np.resize(levels, k // 32))).repeat(32)
    a = np.empty((k // 512, 16))
    for p in range(k // 512):
        a[p, :8] = np.random.permutation(np.resize(levels, 8))
        for g in range(8):
            far = levels[np.abs(levels - a[p, g]) >= 10]
            a[p, g + 8] = far[np.random.randint(len(far))]
    return np.exp2(a.ravel()).repeat(32)


def f64(x):
    return np.asarray(x).astype(np.float64)


def striped(idx):
    return np.tile(idx.reshape(-1, 16).T, (8, 1)).astype(np.uint16)


def unstriped(offs):
    return offs[:16].T.reshape(-1).astype(np.int64)


def striped8(idx):
    return np.concatenate([x.reshape(-1, 16).T for x in idx]).astype(np.uint16)


def runs(offs, k):
    lists = np.stack([offs[16 * r : 16 * r + 16].T.reshape(-1) for r in range(8)]).astype(np.int64)
    return lists[np.arange(k) % 512 // 64]


def pack_weight(w):
    k, n = w.shape
    w = f64(np.asarray(w, np.float32).astype(ml_dtypes.bfloat16)).reshape(k // 32, 32, n)
    amax = np.abs(w).max(1)
    byte = np.clip(np.where(amax > 0, np.frexp(amax)[1] - 1 + 127 - 7, 1), 1, 254)
    scaled = (w * np.exp2(127.0 - byte)[:, None, :]).reshape(k, n).astype(np.float32)
    words = np.ascontiguousarray(scaled.reshape(k // 512, 128, 4, n).transpose(0, 1, 3, 2)).astype(ml_dtypes.float8_e4m3fn).view(np.uint8)
    return words, np.ascontiguousarray(byte.astype(np.uint8).reshape(k // 512, 16, n))


def unpack_weight(words, scales):
    g, p, n, _ = words.shape
    vals = np.ascontiguousarray(words).view(ml_dtypes.float8_e4m3fn).astype(np.float64) * np.repeat(np.exp2(scales.astype(np.float64) - 127.0), 8, axis=1)[..., None]
    return vals.transpose(0, 1, 3, 2).reshape(g * 512, n)


K, T, S, V, H, W, J, G = 512, 2048, 512, 512, 512, 2048, 512, 1024


def setup_inputs():
    n = np.random.standard_normal
    s = mx_kscale(K)[:, None]
    u = mx_kscale(S)
    packed_xT = pack_weight(n((K, T)) * s)
    return {
        "x_words": packed_xT[0],
        "x_scales": packed_xT[1],
        "w1": (n((K, H)) / np.sqrt(K) / s).astype(np.float32),
        "w2": (n((K, H)) / np.sqrt(K) / s).astype(np.float32),
        "tab": np.random.uniform(0.4, 1.4, (H, J)).astype(np.float32),
        "ga": (np.random.uniform(0.5, 1.5, (H, 1)) * u[:, None]).astype(np.float32),
        "gb": (np.random.uniform(0.5, 1.5, (H, 1)) / u[:, None]).astype(np.float32),
        "offs": striped8(np.random.randint(0, T, (8, S))),
        "two": striped(np.random.permutation(T)[:V]),
        "n1": striped(np.random.randint(0, S, W)),
        "n2": striped8(np.random.randint(0, J, (8, V))),
        "n3": striped8(np.stack([np.random.permutation(V) for _ in range(8)])),
        "n4": striped(np.random.randint(0, V, G)),
    }


def reference(x_words, x_scales, w1, w2, tab, ga, gb, offs, two, n1, n2, n3, n4):
    xq = unpack_weight(x_words, x_scales)[np.arange(K)[:, None], runs(offs, K)]
    a = mxq(f64(w1), 0, "e4m3").T @ xq
    ex = np.exp(a)
    mb = ex[:, unstriped(n1)]
    ms = mb.reshape(H, S, 4).sum(axis=2)
    z = f64(ga) * (np.log(ms + ex) - a)
    x_two = unpack_weight(x_words, x_scales)[:, unstriped(two)]
    b = mxq(f64(w2), 0, "e4m3").T @ x_two
    z2 = f64(gb) * (b * (f64(tab)[np.arange(H)[:, None], runs(n2, H)]) - (0.5 * (b[np.arange(H)[:, None], runs(n3, H)])))
    s = 0.0625 * ((mxq(z, 0, "e4m3").T @ mxq(z2, 0, "e4m3")))
    mb2 = s[:, unstriped(n4)]
    ms2 = mb2.reshape(S, V, 2).sum(axis=2)
    mx = mb2.reshape(S, V, 2).max(axis=2)
    return ms2 - np.maximum(s, mx)

@@ -1,0 +1,264 @@
+from contextlib import ExitStack
+
+import concourse.mybir as mybir
+from concourse.masks import make_identity
+
+F32 = mybir.dt.float32
+BF16 = mybir.dt.bfloat16
+I32 = mybir.dt.int32
+U32 = mybir.dt.uint32
+U16 = mybir.dt.uint16
+U8 = mybir.dt.uint8
+FP8X4 = mybir.dt.float8_e4m3fn_x4
+ALU = mybir.AluOpType
+ACT = mybir.ActivationFunctionType
+
+P = 128
+PACK = 4
+T = 2048
+N = 512
+SPARE = 32
+PER_COLUMN = 16
+FLOPS = 3 * 2 * 512 * 512 * 512
+
+
+def entries(lists, first, count):
+    return lists[:, first // PER_COLUMN : (first + count) // PER_COLUMN]
+
+
+def tile_picked_hkqglsekindggpair_none_p_kernel(
+    tc, x_words, x_scales, w1, w2, tab, ga, gb, offs, two, n1, n2, n3, n4, out
+):
+    nc = tc.nc
+    with ExitStack() as ctx:
+        keep = ctx.enter_context(tc.tile_pool(name="keep", bufs=1))
+        ring = ctx.enter_context(tc.tile_pool(name="ring", bufs=2))
+        members = ctx.enter_context(tc.tile_pool(name="members", bufs=8))
+        products = ctx.enter_context(tc.psum_pool(name="products", bufs=4))
+        turned = ctx.enter_context(tc.psum_pool(name="turned", bufs=4))
+
+        def load_list(lists, name):
+            held = keep.tile(list(lists.shape), U16, name=name)
+            nc.sync.dma_start(held[:], lists)
+            return held
+
+        byte_table = keep.tile([P, T], U8, align_bytes=64)
+        nc.gpsimd.memset(byte_table[:].bitcast(I32), 0)
+        offs_sb = load_list(offs, "offs_sb")
+
+        def load_half(w, h, name):
+            raw = keep.tile([P, PACK, N // 2], F32, align_bytes=64, name="%s_raw%d" % (name, h))
+            nc.sync.dma_start(raw[:], w.rearrange("(p j) c -> p j c", j=PACK)[:, :, h * 256 : (h + 1) * 256])
+            return raw
+
+        w1_raw = [load_half(w1, 0, "w1")]
+        scale_rows = x_scales[0].bitcast(I32)
+        byte_rows = byte_table[:].bitcast(I32)
+        for j in range(4):
+            nc.sync.dma_start(byte_rows[16 * (j // 2) + j : P : 32, :], scale_rows[j:16:4, :])
+        word_table = keep.tile([P, T], I32, align_bytes=64)
+        nc.sync.dma_start(word_table[:], x_words[0].rearrange("p n r -> p (n r)").bitcast(I32))
+        w1_raw.append(load_half(w1, 1, "w1"))
+        two_sb = load_list(two, "two_sb")
+
+        identity = keep.tile([P, P], F32)
+        make_identity(nc, identity[:])
+        ex = [keep.tile([P, N + SPARE], F32, name="ex%d" % t) for t in range(PACK)]
+        s_sb = [keep.tile([P, N + SPARE], F32, name="s%d" % c) for c in range(4)]
+        for window in ex + s_sb:
+            nc.gpsimd.memset(window[:, N:], 0.0)
+
+        def pick_scales(lists, name, tag):
+            picked_bytes = keep.tile([P, N], U8, align_bytes=64, name=name + "_bytes", tag=tag)
+            nc.vector.tensor_copy(picked_bytes[:], byte_table[:].indirect(lists[:]))
+            scales = keep.tile([P, N], U8, align_bytes=64, name=name + "_scales")
+            nc.vector.tensor_copy(scales[:].bitcast(I32), picked_bytes[:].bitcast(I32))
+            for j in (2, 3):
+                nc.sync.dma_start(
+                    scales[:].bitcast(I32)[j:P:32, :], picked_bytes[:].bitcast(I32)[16 + j : P : 32, :]
+                )
+            return scales
+
+        def pick_words(lists, name, tag):
+            picked_words = keep.tile([P, N], U32, align_bytes=64, name=name + "_words", tag=tag)
+            nc.vector.tensor_copy(picked_words[:], word_table[:].bitcast(U32).indirect(lists[:]))
+            return picked_words
+
+        def quantise_weight(halves, name, shares):
+            grouped = keep.tile([P, PACK, P, PACK], BF16, align_bytes=64, name=name + "_grouped")
+            for cast, first, count in shares:
+                raw = halves[first // 64][:].rearrange("p j (m t) -> p m t j", t=PACK)
+                cast(
+                    grouped[:, :, first : first + count, :].rearrange("p t m j -> p m t j"),
+                    raw[:, first % 64 : first % 64 + count, :, :],
+                )
+            words = keep.tile([P, N], U32, align_bytes=64, name=name + "_words")
+            scales = keep.tile([P, N], U8, align_bytes=64, name=name + "_scales")
+            for t in range(PACK):
+                cols = slice(t * P, (t + 1) * P)
+                nc.vector.quantize_mx(
+                    out=words[:, cols].bitcast(FP8X4),
+                    scales=scales[:, cols],
+                    in_=grouped[:, t, :, :].rearrange("p m j -> p (m j)"),
+                )
+            return words, scales
+
+        def product(pool, l_words, l_scales, r_words, r_scales):
+            bank = pool.tile([P, N], F32, name="bank")
+            nc.tensor.matmul_mx(
+                out=bank[:],
+                lhsT=l_words.bitcast(FP8X4),
+                lhsT_scale=l_scales,
+                rhs=r_words.bitcast(FP8X4),
+                rhs_scale=r_scales,
+                start=True,
+                stop=True,
+            )
+            return bank
+
+        def scalar_gather(dst, src):
+            nc.scalar.activation(dst, src, ACT.Copy)
+
+        vector_gather = nc.vector.tensor_copy
+        xa_scales = pick_scales(offs_sb, "xa", "xa_bytes")
+        xa_words = pick_words(offs_sb, "xa", "xa_words")
+        w1_words, w1_scales = quantise_weight(
+            w1_raw, "w1", ((scalar_gather, 0, 64), (scalar_gather, 64, 32), (vector_gather, 96, 32))
+        )
+        xb_scales = pick_scales(two_sb, "xb", "w1_raw1")
+        xb_words = pick_words(two_sb, "xb", "w1_grouped")
+
+        w2_raw = [load_half(w2, h, "w2") for h in range(2)]
+        n1_sb = load_list(n1, "n1_sb")
+        gb_sb = keep.tile([P, PACK], F32)
+        nc.sync.dma_start(gb_sb[:], gb.rearrange("(p t) o -> p (t o)", t=PACK))
+        tab_sb = [keep.tile([P, N], F32, name="tab%d" % t) for t in range(PACK)]
+        for h in range(2):
+            tab_raw = keep.tile([P, 2, N], F32, name="tab_raw%d" % h)
+            nc.sync.dma_start(tab_raw[:], tab.rearrange("(p t) c -> p t c", t=PACK)[:, 2 * h : 2 * h + 2, :])
+            for t in range(2):
+                nc.gpsimd.tensor_scalar(tab_sb[2 * h + t][:], tab_raw[:, t, :], 2.0, 0.0, ALU.mult, ALU.add)
+        n2_sb = load_list(n2, "n2_sb")
+        n3_sb = load_list(n3, "n3_sb")
+        ga_sb = keep.tile([P, PACK], F32)
+        nc.sync.dma_start(ga_sb[:], ga.rearrange("(p t) o -> p (t o)", t=PACK))
+        n4_sb = load_list(n4, "n4_sb")
+
+        a_banks = []
+        for t in range(PACK):
+            cols = slice(t * P, (t + 1) * P)
+            a_banks.append(product(products, w1_words[:, cols], w1_scales[:, cols], xa_words[:], xa_scales[:]))
+            nc.scalar.activation(ex[t][:, :N], a_banks[t][:], ACT.Exp)
+
+        w2_words, w2_scales = quantise_weight(w2_raw, "w2", ((vector_gather, 0, 64), (vector_gather, 64, 64)))
+        less_half = [keep.tile([P, N], F32, name="less_half%d" % t) for t in range(PACK)]
+        for t in range(PACK):
+            cols = slice(t * P, (t + 1) * P)
+            b_bank = product(turned, w2_words[:, cols], w2_scales[:, cols], xb_words[:], xb_scales[:])
+            nc.vector.tensor_scalar(less_half[t][:], b_bank[:], gb_sb[:, t : t + 1], -0.5, ALU.mult, ALU.mult)
+
+        weighted_a = [keep.tile([P, N], F32, name="ga_a%d" % t) for t in range(PACK)]
+
+        def sum_members(c, on_vector):
+            total = turned.tile([P, PACK, P], F32, name="bank")
+            for t in range(PACK):
+                mb = members.tile([P, N], F32, name="mb")
+                gather = vector_gather if t < on_vector else scalar_gather
+                gather(mb[:], ex[t][:].indirect(entries(n1_sb, c * N, N)))
+                addends = [ex[t][:, c * P : (c + 1) * P]] + [mb[:, u:N:4] for u in range(4)]
+                for u, addend in enumerate(addends):
+                    nc.tensor.matmul(
+                        total[:, t, :], addend, identity[:], start=(u == 0), stop=(u == 4), is_transpose=True
+                    )
+            return total
+
+        def logarithm(total):
+            log_turned = ring.tile([P, PACK, P], F32, name="log_turned")
+            nc.scalar.activation(log_turned[:], total[:], ACT.Ln)
+            log_bank = turned.tile([P, PACK, P], F32, name="bank")
+            for t in range(PACK):
+                nc.tensor.transpose(log_bank[:, t, :], log_turned[:, t, :], identity[:])
+            return log_bank
+
+        def quantise_planes(planes, width, name):
+            grouped = keep.tile([P, width, PACK], BF16, align_bytes=64, name=name + "_grouped")
+            nc.vector.tensor_copy(
+                grouped[:].rearrange("p (c i) t -> p c t i", i=4),
+                planes[:].rearrange("p t (c i) -> p c t i", i=4),
+            )
+            words = keep.tile([P, width], U32, align_bytes=64, name=name + "_words")
+            scales = keep.tile([P, width], U8, align_bytes=64, name=name + "_scales")
+            nc.vector.quantize_mx(
+                out=words[:].bitcast(FP8X4), scales=scales[:], in_=grouped[:].rearrange("p c t -> p (c t)")
+            )
+            return words, scales
+
+        def finish_z(c, log_bank):
+            z = ring.tile([P, PACK, P], F32, name="z")
+            for t in range(PACK):
+                nc.vector.scalar_tensor_tensor(
+                    z[:, t, :],
+                    log_bank[:, t, :],
+                    ga_sb[:, t : t + 1],
+                    weighted_a[t][:, c * P : (c + 1) * P],
+                    ALU.mult,
+                    ALU.subtract,
+                )
+            return quantise_planes(z, P, "zblock%d" % c)
+
+        z2 = keep.tile([P, PACK, N], F32)
+
+        def make_z2(t):
+            kind = ring.tile([P, N], F32, name="kind")
+            for first in (0, 256):
+                part = slice(first, first + 256)
+                nc.vector.tensor_tensor(
+                    kind[:, part], tab_sb[t][:].indirect(entries(n2_sb, first, 256)), less_half[t][:, part], ALU.mult
+                )
+            for first in (0, 256):
+                part = slice(first, first + 256)
+                nc.vector.tensor_tensor(
+                    z2[:, t, part], less_half[t][:].indirect(entries(n3_sb, first, 256)), kind[:, part], ALU.subtract
+                )
+
+        def product_s(c, z_c, z2_q):
+            s_bank = product(products, z_c[0][:], z_c[1][:], z2_q[0][:], z2_q[1][:])
+            nc.scalar.activation(s_sb[c][:, :N], s_bank[:], ACT.Copy, scale=0.0625)
+
+        def fetch_pairs(c, h, gather):
+            pairs = members.tile([P, N // 2, 2], F32, name="pairs")
+            gather(pairs[:].rearrange("p v u -> p (v u)"), s_sb[c][:].indirect(entries(n4_sb, h * N, N)))
+            return pairs
+
+        def finish_out(c, h, pairs):
+            part = slice(h * 256, (h + 1) * 256)
+            gap = ring.tile([P, N // 2], F32, name="gap")
+            nc.vector.tensor_tensor(gap[:], pairs[:, :, 0], s_sb[c][:, part], ALU.subtract)
+            lower = ring.tile([P, N // 2], F32, name="lower")
+            nc.vector.scalar_tensor_tensor(lower[:], gap[:], 0.0, pairs[:, :, 1], ALU.min, ALU.add)
+            result = members.tile([P, N // 2], F32, name="result")
+            nc.vector.tensor_tensor(result[:], lower[:], pairs[:, :, 0], ALU.min)
+            nc.sync.dma_start(out[c * P : (c + 1) * P, part], result[:])
+
+        totals = [sum_members(0, 0), sum_members(1, 0)]
+        for t in range(PACK):
+            make_z2(t)
+        logs = [logarithm(totals[0])]
+        totals.append(sum_members(2, 0))
+        logs.append(logarithm(totals[1]))
+        totals.append(sum_members(3, 0))
+        for t in range(PACK):
+            nc.vector.tensor_scalar(weighted_a[t][:], a_banks[t][:], ga_sb[:, t : t + 1], None, ALU.mult)
+        z2_q = quantise_planes(z2, N, "z2")
+        zq = [finish_z(0, logs[0])]
+        logs.append(logarithm(totals[2]))
+        zq.append(finish_z(1, logs[1]))
+        logs.append(logarithm(totals[3]))
+        zq.append(finish_z(2, logs[2]))
+        zq.append(finish_z(3, logs[3]))
+        product_s(0, zq[0], z2_q)
+        for c in range(4):
+            if c < 3:
+                product_s(c + 1, zq[c + 1], z2_q)
+            for h in range(2):
+                finish_out(c, h, fetch_pairs(c, h, vector_gather if (c, h) in ((2, 1),) else scalar_gather))

@@ -18,6 +18,8 @@ PACK = 4
 T = 2048
 N = 512
 SPARE = 32
+HEAD = 32
+SCALAR_SHARE = 32
 PER_COLUMN = 16
 FLOPS = 3 * 2 * 512 * 512 * 512
 
@@ -34,8 +36,8 @@ def tile_picked_hkqglsekindggpair_none_p_kernel(
         keep = ctx.enter_context(tc.tile_pool(name="keep", bufs=1))
         ring = ctx.enter_context(tc.tile_pool(name="ring", bufs=2))
         members = ctx.enter_context(tc.tile_pool(name="members", bufs=8))
-        products = ctx.enter_context(tc.psum_pool(name="products", bufs=4))
-        turned = ctx.enter_context(tc.psum_pool(name="turned", bufs=4))
+        psum = ctx.enter_context(tc.psum_pool(name="psum", bufs=1))
+        banks = [psum.tile([P, N], F32, name="bank%d" % i) for i in range(8)]
 
         def load_list(lists, name):
             held = keep.tile(list(lists.shape), U16, name=name)
@@ -46,20 +48,23 @@ def tile_picked_hkqglsekindggpair_none_p_kernel(
         nc.gpsimd.memset(byte_table[:].bitcast(I32), 0)
         offs_sb = load_list(offs, "offs_sb")
 
-        def load_half(w, h, name):
-            raw = keep.tile([P, PACK, N // 2], F32, align_bytes=64, name="%s_raw%d" % (name, h))
-            nc.sync.dma_start(raw[:], w.rearrange("(p j) c -> p j c", j=PACK)[:, :, h * 256 : (h + 1) * 256])
-            return raw
+        def load_columns(w, first, count, name):
+            raw = keep.tile([P, PACK, PACK * count], F32, name="%s_raw%d" % (name, first))
+            nc.sync.dma_start(
+                raw[:], w.rearrange("(p j) c -> p j c", j=PACK)[:, :, PACK * first : PACK * (first + count)]
+            )
+            return raw[:].rearrange("p j (m t) -> p m t j", t=PACK)
 
-        w1_raw = [load_half(w1, 0, "w1")]
+        w1_head = load_columns(w1, 0, HEAD, "w1")
+        two_sb = load_list(two, "two_sb")
         scale_rows = x_scales[0].bitcast(I32)
         byte_rows = byte_table[:].bitcast(I32)
         for j in range(4):
             nc.sync.dma_start(byte_rows[16 * (j // 2) + j : P : 32, :], scale_rows[j:16:4, :])
         word_table = keep.tile([P, T], I32, align_bytes=64)
         nc.sync.dma_start(word_table[:], x_words[0].rearrange("p n r -> p (n r)").bitcast(I32))
-        w1_raw.append(load_half(w1, 1, "w1"))
-        two_sb = load_list(two, "two_sb")
+        w1_rest = load_columns(w1, HEAD, P - HEAD, "w1")
+        w2_raw = [load_columns(w2, 0, P // 2, "w2")]
 
         identity = keep.tile([P, P], F32)
         make_identity(nc, identity[:])
@@ -68,8 +73,8 @@ def tile_picked_hkqglsekindggpair_none_p_kernel(
         for window in ex + s_sb:
             nc.gpsimd.memset(window[:, N:], 0.0)
 
-        def pick_scales(lists, name, tag):
-            picked_bytes = keep.tile([P, N], U8, align_bytes=64, name=name + "_bytes", tag=tag)
+        def pick_scales(lists, name):
+            picked_bytes = keep.tile([P, N], U8, align_bytes=64, name=name + "_bytes")
             nc.vector.tensor_copy(picked_bytes[:], byte_table[:].indirect(lists[:]))
             scales = keep.tile([P, N], U8, align_bytes=64, name=name + "_scales")
             nc.vector.tensor_copy(scales[:].bitcast(I32), picked_bytes[:].bitcast(I32))
@@ -84,14 +89,13 @@ def tile_picked_hkqglsekindggpair_none_p_kernel(
             nc.vector.tensor_copy(picked_words[:], word_table[:].bitcast(U32).indirect(lists[:]))
             return picked_words
 
-        def quantise_weight(halves, name, shares):
+        def quantise_weight(name, shares):
             grouped = keep.tile([P, PACK, P, PACK], BF16, align_bytes=64, name=name + "_grouped")
-            for cast, first, count in shares:
-                raw = halves[first // 64][:].rearrange("p j (m t) -> p m t j", t=PACK)
-                cast(
-                    grouped[:, :, first : first + count, :].rearrange("p t m j -> p m t j"),
-                    raw[:, first % 64 : first % 64 + count, :, :],
-                )
+            first = 0
+            for cast, raw in shares:
+                count = raw.shape[1]
+                cast(grouped[:, :, first : first + count, :].rearrange("p t m j -> p m t j"), raw)
+                first = first + count
             words = keep.tile([P, N], U32, align_bytes=64, name=name + "_words")
             scales = keep.tile([P, N], U8, align_bytes=64, name=name + "_scales")
             for t in range(PACK):
@@ -103,8 +107,7 @@ def tile_picked_hkqglsekindggpair_none_p_kernel(
                 )
             return words, scales
 
-        def product(pool, l_words, l_scales, r_words, r_scales):
-            bank = pool.tile([P, N], F32, name="bank")
+        def product(bank, l_words, l_scales, r_words, r_scales):
             nc.tensor.matmul_mx(
                 out=bank[:],
                 lhsT=l_words.bitcast(FP8X4),
@@ -120,15 +123,20 @@ def tile_picked_hkqglsekindggpair_none_p_kernel(
             nc.scalar.activation(dst, src, ACT.Copy)
 
         vector_gather = nc.vector.tensor_copy
-        xa_scales = pick_scales(offs_sb, "xa", "xa_bytes")
+        xa_scales = pick_scales(offs_sb, "xa")
+        xb_scales = pick_scales(two_sb, "xb")
         xa_words = pick_words(offs_sb, "xa", "xa_words")
         w1_words, w1_scales = quantise_weight(
-            w1_raw, "w1", ((scalar_gather, 0, 64), (scalar_gather, 64, 32), (vector_gather, 96, 32))
+            "w1",
+            (
+                (scalar_gather, w1_head),
+                (scalar_gather, w1_rest[:, :SCALAR_SHARE, :, :]),
+                (vector_gather, w1_rest[:, SCALAR_SHARE:, :, :]),
+            ),
         )
-        xb_scales = pick_scales(two_sb, "xb", "w1_raw1")
         xb_words = pick_words(two_sb, "xb", "w1_grouped")
 
-        w2_raw = [load_half(w2, h, "w2") for h in range(2)]
+        w2_raw.append(load_columns(w2, P // 2, P // 2, "w2"))
         n1_sb = load_list(n1, "n1_sb")
         gb_sb = keep.tile([P, PACK], F32)
         nc.sync.dma_start(gb_sb[:], gb.rearrange("(p t) o -> p (t o)", t=PACK))
@@ -147,24 +155,27 @@ def tile_picked_hkqglsekindggpair_none_p_kernel(
         a_banks = []
         for t in range(PACK):
             cols = slice(t * P, (t + 1) * P)
-            a_banks.append(product(products, w1_words[:, cols], w1_scales[:, cols], xa_words[:], xa_scales[:]))
+            a_banks.append(product(banks[t], w1_words[:, cols], w1_scales[:, cols], xa_words[:], xa_scales[:]))
             nc.scalar.activation(ex[t][:, :N], a_banks[t][:], ACT.Exp)
 
-        w2_words, w2_scales = quantise_weight(w2_raw, "w2", ((vector_gather, 0, 64), (vector_gather, 64, 64)))
+        w2_words, w2_scales = quantise_weight("w2", [(vector_gather, raw) for raw in w2_raw])
         less_half = [keep.tile([P, N], F32, name="less_half%d" % t) for t in range(PACK)]
         for t in range(PACK):
             cols = slice(t * P, (t + 1) * P)
-            b_bank = product(turned, w2_words[:, cols], w2_scales[:, cols], xb_words[:], xb_scales[:])
+            b_bank = product(banks[4 + t % 2], w2_words[:, cols], w2_scales[:, cols], xb_words[:], xb_scales[:])
             nc.vector.tensor_scalar(less_half[t][:], b_bank[:], gb_sb[:, t : t + 1], -0.5, ALU.mult, ALU.mult)
 
         weighted_a = [keep.tile([P, N], F32, name="ga_a%d" % t) for t in range(PACK)]
 
-        def sum_members(c, on_vector):
-            total = turned.tile([P, PACK, P], F32, name="bank")
+        def fetch_members(c, t, gather):
+            mb = members.tile([P, N], F32, name="mb", bufs=16)
+            gather(mb[:], ex[t][:].indirect(entries(n1_sb, c * N, N)))
+            return mb
+
+        def sum_members(c, fetched, bank):
+            total = bank[:].rearrange("p (t j) -> p t j", t=PACK)
             for t in range(PACK):
-                mb = members.tile([P, N], F32, name="mb")
-                gather = vector_gather if t < on_vector else scalar_gather
-                gather(mb[:], ex[t][:].indirect(entries(n1_sb, c * N, N)))
+                mb = fetched[t] if t in fetched else fetch_members(c, t, scalar_gather)
                 addends = [ex[t][:, c * P : (c + 1) * P]] + [mb[:, u:N:4] for u in range(4)]
                 for u, addend in enumerate(addends):
                     nc.tensor.matmul(
@@ -172,10 +183,13 @@ def tile_picked_hkqglsekindggpair_none_p_kernel(
                     )
             return total
 
-        def logarithm(total):
+        def weigh_a(t):
+            nc.scalar.activation(weighted_a[t][:], a_banks[t][:], ACT.Copy, scale=ga_sb[:, t : t + 1])
+
+        def logarithm(c, total):
             log_turned = ring.tile([P, PACK, P], F32, name="log_turned")
-            nc.scalar.activation(log_turned[:], total[:], ACT.Ln)
-            log_bank = turned.tile([P, PACK, P], F32, name="bank")
+            nc.scalar.activation(log_turned[:], total, ACT.Ln)
+            log_bank = banks[c][:].rearrange("p (t j) -> p t j", t=PACK)
             for t in range(PACK):
                 nc.tensor.transpose(log_bank[:, t, :], log_turned[:, t, :], identity[:])
             return log_bank
@@ -221,9 +235,12 @@ def tile_picked_hkqglsekindggpair_none_p_kernel(
                     z2[:, t, part], less_half[t][:].indirect(entries(n3_sb, first, 256)), kind[:, part], ALU.subtract
                 )
 
-        def product_s(c, z_c, z2_q):
-            s_bank = product(products, z_c[0][:], z_c[1][:], z2_q[0][:], z2_q[1][:])
-            nc.scalar.activation(s_sb[c][:, :N], s_bank[:], ACT.Copy, scale=0.0625)
+        def product_s(c, z_c, z2_q, bank, on_vector):
+            s_bank = product(bank, z_c[0][:], z_c[1][:], z2_q[0][:], z2_q[1][:])
+            if on_vector:
+                nc.vector.tensor_scalar(s_sb[c][:, :N], s_bank[:], 0.0625, None, ALU.mult)
+            else:
+                nc.scalar.activation(s_sb[c][:, :N], s_bank[:], ACT.Copy, scale=0.0625)
 
         def fetch_pairs(c, h, gather):
             pairs = members.tile([P, N // 2, 2], F32, name="pairs")
@@ -240,25 +257,25 @@ def tile_picked_hkqglsekindggpair_none_p_kernel(
             nc.vector.tensor_tensor(result[:], lower[:], pairs[:, :, 0], ALU.min)
             nc.sync.dma_start(out[c * P : (c + 1) * P, part], result[:])
 
-        totals = [sum_members(0, 0), sum_members(1, 0)]
+        early = {t: fetch_members(2, t, vector_gather) for t in range(2)}
+        totals = [sum_members(0, {}, banks[6]), sum_members(1, {}, banks[7])]
         for t in range(PACK):
             make_z2(t)
-        logs = [logarithm(totals[0])]
-        totals.append(sum_members(2, 0))
-        logs.append(logarithm(totals[1]))
-        totals.append(sum_members(3, 0))
         for t in range(PACK):
-            nc.vector.tensor_scalar(weighted_a[t][:], a_banks[t][:], ga_sb[:, t : t + 1], None, ALU.mult)
+            weigh_a(t)
+        logs = [logarithm(0, totals[0])]
+        totals.append(sum_members(2, early, banks[4]))
+        logs.append(logarithm(1, totals[1]))
+        totals.append(sum_members(3, {}, banks[5]))
+        logs.append(logarithm(2, totals[2]))
+        logs.append(logarithm(3, totals[3]))
         z2_q = quantise_planes(z2, N, "z2")
-        zq = [finish_z(0, logs[0])]
-        logs.append(logarithm(totals[2]))
-        zq.append(finish_z(1, logs[1]))
-        logs.append(logarithm(totals[3]))
-        zq.append(finish_z(2, logs[2]))
-        zq.append(finish_z(3, logs[3]))
-        product_s(0, zq[0], z2_q)
+        pairs = {}
         for c in range(4):
-            if c < 3:
-                product_s(c + 1, zq[c + 1], z2_q)
+            product_s(c, finish_z(c, logs[c]), z2_q, banks[(6, 7, 4, 5)[c]], c in (0,))
             for h in range(2):
-                finish_out(c, h, fetch_pairs(c, h, vector_gather if (c, h) in ((2, 1),) else scalar_gather))
+                if (c, h) in ((0,0),):
+                    pairs[c, h] = fetch_pairs(c, h, vector_gather)
+        for c in range(4):
+            for h in range(2):
+                finish_out(c, h, pairs[c, h] if (c, h) in pairs else fetch_pairs(c, h, scalar_gather))

@@ -15,17 +15,22 @@ ACT = mybir.ActivationFunctionType
 
 P = 128
 PACK = 4
-T = 2048
+TOKENS = 2048
 N = 512
+HALF = N // 2
+BLOCKS = N // P
+MEMBERS = 4
+GROUP = 16
+QUADRANT = 32
 SPARE = 32
-HEAD = 32
-SCALAR_SHARE = 32
-PER_COLUMN = 16
+W1_ON_SCALAR = 40
+W2_ON_SCALAR = 32
+PLANES_ON_VECTOR = 3
 FLOPS = 3 * 2 * 512 * 512 * 512
 
 
-def entries(lists, first, count):
-    return lists[:, first // PER_COLUMN : (first + count) // PER_COLUMN]
+def entries(lists, start, count):
+    return lists[:, start // GROUP : (start + count) // GROUP]
 
 
 def tile_picked_hkqglsekindggpair_none_p_kernel(
@@ -35,74 +40,78 @@ def tile_picked_hkqglsekindggpair_none_p_kernel(
     with ExitStack() as ctx:
         keep = ctx.enter_context(tc.tile_pool(name="keep", bufs=1))
         ring = ctx.enter_context(tc.tile_pool(name="ring", bufs=2))
-        members = ctx.enter_context(tc.tile_pool(name="members", bufs=8))
         psum = ctx.enter_context(tc.psum_pool(name="psum", bufs=1))
-        banks = [psum.tile([P, N], F32, name="bank%d" % i) for i in range(8)]
+        first = [psum.tile([P, N], F32, name="first%d" % i) for i in range(PACK)]
+        second = [psum.tile([P, N], F32, name="second%d" % i) for i in range(PACK)]
+
+        def scalar_copy(dst, src):
+            nc.scalar.activation(dst, src, ACT.Copy)
+
+        vector_copy = nc.vector.tensor_copy
 
         def load_list(lists, name):
             held = keep.tile(list(lists.shape), U16, name=name)
             nc.sync.dma_start(held[:], lists)
             return held
 
-        byte_table = keep.tile([P, T], U8, align_bytes=64)
-        nc.gpsimd.memset(byte_table[:].bitcast(I32), 0)
-        offs_sb = load_list(offs, "offs_sb")
+        def load_factor(factor, name):
+            held = keep.tile([P, PACK], F32, name=name)
+            nc.sync.dma_start(held[:], factor.rearrange("(p t) o -> p (t o)", t=PACK))
+            return held
 
-        def load_columns(w, first, count, name):
-            raw = keep.tile([P, PACK, PACK * count], F32, name="%s_raw%d" % (name, first))
-            nc.sync.dma_start(
-                raw[:], w.rearrange("(p j) c -> p j c", j=PACK)[:, :, PACK * first : PACK * (first + count)]
-            )
+        def dealt(raw):
             return raw[:].rearrange("p j (m t) -> p m t j", t=PACK)
 
-        w1_head = load_columns(w1, 0, HEAD, "w1")
+        def gathered_row(j):
+            return slice(GROUP * (j // 2) + j, P, QUADRANT)
+
+        byte_table = keep.tile([P, TOKENS], U8, align_bytes=64)
+        nc.gpsimd.memset(byte_table[:].bitcast(I32), 0)
+        offs_sb = load_list(offs, "offs_sb")
+        w1_raw = keep.tile([P, PACK, N], F32)
+        w1_rows = w1.rearrange("(p j) c -> p j c", j=PACK)
+        nc.sync.dma_start(w1_raw[:, :1, :], w1_rows[:, :1, :])
         two_sb = load_list(two, "two_sb")
-        scale_rows = x_scales[0].bitcast(I32)
-        byte_rows = byte_table[:].bitcast(I32)
         for j in range(4):
-            nc.sync.dma_start(byte_rows[16 * (j // 2) + j : P : 32, :], scale_rows[j:16:4, :])
-        word_table = keep.tile([P, T], I32, align_bytes=64)
+            nc.sync.dma_start(byte_table[:].bitcast(I32)[gathered_row(j), :], x_scales[0].bitcast(I32)[j:16:4, :])
+        word_table = keep.tile([P, TOKENS], I32, align_bytes=64)
         nc.sync.dma_start(word_table[:], x_words[0].rearrange("p n r -> p (n r)").bitcast(I32))
-        w1_rest = load_columns(w1, HEAD, P - HEAD, "w1")
-        w2_raw = [load_columns(w2, 0, P // 2, "w2")]
+        nc.sync.dma_start(w1_raw[:, 1:, :], w1_rows[:, 1:, :])
 
         identity = keep.tile([P, P], F32)
         make_identity(nc, identity[:])
         ex = [keep.tile([P, N + SPARE], F32, name="ex%d" % t) for t in range(PACK)]
-        s_sb = [keep.tile([P, N + SPARE], F32, name="s%d" % c) for c in range(4)]
+        s_sb = [keep.tile([P, N + SPARE], F32, name="s%d" % c) for c in range(BLOCKS)]
         for window in ex + s_sb:
             nc.gpsimd.memset(window[:, N:], 0.0)
 
         def pick_scales(lists, name):
-            picked_bytes = keep.tile([P, N], U8, align_bytes=64, name=name + "_bytes")
-            nc.vector.tensor_copy(picked_bytes[:], byte_table[:].indirect(lists[:]))
+            picked = keep.tile([P, N], U8, align_bytes=64, name=name + "_bytes")
+            nc.vector.tensor_copy(picked[:], byte_table[:].indirect(lists[:]))
             scales = keep.tile([P, N], U8, align_bytes=64, name=name + "_scales")
-            nc.vector.tensor_copy(scales[:].bitcast(I32), picked_bytes[:].bitcast(I32))
+            nc.vector.tensor_copy(scales[:].bitcast(I32), picked[:].bitcast(I32))
             for j in (2, 3):
-                nc.sync.dma_start(
-                    scales[:].bitcast(I32)[j:P:32, :], picked_bytes[:].bitcast(I32)[16 + j : P : 32, :]
-                )
+                nc.sync.dma_start(scales[:].bitcast(I32)[j:P:QUADRANT, :], picked[:].bitcast(I32)[gathered_row(j), :])
             return scales
 
-        def pick_words(lists, name, tag):
-            picked_words = keep.tile([P, N], U32, align_bytes=64, name=name + "_words", tag=tag)
-            nc.vector.tensor_copy(picked_words[:], word_table[:].bitcast(U32).indirect(lists[:]))
-            return picked_words
+        def pick_words(lists, tag):
+            picked = keep.tile([P, N], U32, align_bytes=64, name="picked_words", tag=tag)
+            nc.vector.tensor_copy(picked[:], word_table[:].bitcast(U32).indirect(lists[:]))
+            return picked
 
         def quantise_weight(name, shares):
             grouped = keep.tile([P, PACK, P, PACK], BF16, align_bytes=64, name=name + "_grouped")
-            first = 0
-            for cast, raw in shares:
+            m = 0
+            for copy_share, raw in shares:
                 count = raw.shape[1]
-                cast(grouped[:, :, first : first + count, :].rearrange("p t m j -> p m t j"), raw)
-                first = first + count
-            words = keep.tile([P, N], U32, align_bytes=64, name=name + "_words")
-            scales = keep.tile([P, N], U8, align_bytes=64, name=name + "_scales")
+                copy_share(grouped[:, :, m : m + count, :].rearrange("p t m j -> p m t j"), raw)
+                m = m + count
+            words = keep.tile([P, PACK, P], U32, align_bytes=64, name=name + "_words")
+            scales = keep.tile([P, PACK, P], U8, align_bytes=64, name=name + "_scales")
             for t in range(PACK):
-                cols = slice(t * P, (t + 1) * P)
                 nc.vector.quantize_mx(
-                    out=words[:, cols].bitcast(FP8X4),
-                    scales=scales[:, cols],
+                    out=words[:, t, :].bitcast(FP8X4),
+                    scales=scales[:, t, :],
                     in_=grouped[:, t, :, :].rearrange("p m j -> p (m j)"),
                 )
             return words, scales
@@ -117,82 +126,77 @@ def tile_picked_hkqglsekindggpair_none_p_kernel(
                 start=True,
                 stop=True,
             )
-            return bank
 
-        def scalar_gather(dst, src):
-            nc.scalar.activation(dst, src, ACT.Copy)
+        def load_w2_half(h):
+            raw = keep.tile([P, PACK, HALF], F32, name="w2_raw%d" % h)
+            nc.sync.dma_start(raw[:], w2.rearrange("(p j) c -> p j c", j=PACK)[:, :, h * HALF : (h + 1) * HALF])
+            return dealt(raw)
 
-        vector_gather = nc.vector.tensor_copy
+        w2_low = load_w2_half(0)
         xa_scales = pick_scales(offs_sb, "xa")
         xb_scales = pick_scales(two_sb, "xb")
-        xa_words = pick_words(offs_sb, "xa", "xa_words")
+        xa_words = pick_words(offs_sb, "xa_words")
         w1_words, w1_scales = quantise_weight(
             "w1",
-            (
-                (scalar_gather, w1_head),
-                (scalar_gather, w1_rest[:, :SCALAR_SHARE, :, :]),
-                (vector_gather, w1_rest[:, SCALAR_SHARE:, :, :]),
-            ),
+            ((scalar_copy, dealt(w1_raw)[:, :W1_ON_SCALAR, :, :]), (vector_copy, dealt(w1_raw)[:, W1_ON_SCALAR:, :, :])),
         )
-        xb_words = pick_words(two_sb, "xb", "w1_grouped")
+        xb_words = pick_words(two_sb, "w1_grouped")
 
-        w2_raw.append(load_columns(w2, P // 2, P // 2, "w2"))
+        w2_high = load_w2_half(1)
         n1_sb = load_list(n1, "n1_sb")
-        gb_sb = keep.tile([P, PACK], F32)
-        nc.sync.dma_start(gb_sb[:], gb.rearrange("(p t) o -> p (t o)", t=PACK))
-        tab_sb = [keep.tile([P, N], F32, name="tab%d" % t) for t in range(PACK)]
+        ga_sb = load_factor(ga, "ga_sb")
+        gb_sb = load_factor(gb, "gb_sb")
+        twice_tab = [keep.tile([P, N], F32, name="twice_tab%d" % t) for t in range(PACK)]
         for h in range(2):
             tab_raw = keep.tile([P, 2, N], F32, name="tab_raw%d" % h)
             nc.sync.dma_start(tab_raw[:], tab.rearrange("(p t) c -> p t c", t=PACK)[:, 2 * h : 2 * h + 2, :])
-            for t in range(2):
-                nc.gpsimd.tensor_scalar(tab_sb[2 * h + t][:], tab_raw[:, t, :], 2.0, 0.0, ALU.mult, ALU.add)
+            for u in range(2):
+                nc.gpsimd.tensor_scalar(twice_tab[2 * h + u][:], tab_raw[:, u, :], 2.0, 0.0, ALU.mult, ALU.add)
         n2_sb = load_list(n2, "n2_sb")
         n3_sb = load_list(n3, "n3_sb")
-        ga_sb = keep.tile([P, PACK], F32)
-        nc.sync.dma_start(ga_sb[:], ga.rearrange("(p t) o -> p (t o)", t=PACK))
         n4_sb = load_list(n4, "n4_sb")
 
-        a_banks = []
         for t in range(PACK):
-            cols = slice(t * P, (t + 1) * P)
-            a_banks.append(product(banks[t], w1_words[:, cols], w1_scales[:, cols], xa_words[:], xa_scales[:]))
-            nc.scalar.activation(ex[t][:, :N], a_banks[t][:], ACT.Exp)
+            product(first[t], w1_words[:, t, :], w1_scales[:, t, :], xa_words[:], xa_scales[:])
+            nc.scalar.activation(ex[t][:, :N], first[t][:], ACT.Exp)
 
-        w2_words, w2_scales = quantise_weight("w2", [(vector_gather, raw) for raw in w2_raw])
+        w2_words, w2_scales = quantise_weight(
+            "w2",
+            (
+                (scalar_copy, w2_low[:, :W2_ON_SCALAR, :, :]),
+                (vector_copy, w2_low[:, W2_ON_SCALAR:, :, :]),
+                (vector_copy, w2_high),
+            ),
+        )
         less_half = [keep.tile([P, N], F32, name="less_half%d" % t) for t in range(PACK)]
         for t in range(PACK):
-            cols = slice(t * P, (t + 1) * P)
-            b_bank = product(banks[4 + t % 2], w2_words[:, cols], w2_scales[:, cols], xb_words[:], xb_scales[:])
-            nc.vector.tensor_scalar(less_half[t][:], b_bank[:], gb_sb[:, t : t + 1], -0.5, ALU.mult, ALU.mult)
+            product(second[t], w2_words[:, t, :], w2_scales[:, t, :], xb_words[:], xb_scales[:])
+            nc.vector.tensor_scalar(less_half[t][:], second[t][:], gb_sb[:, t : t + 1], -0.5, ALU.mult, ALU.mult)
 
-        weighted_a = [keep.tile([P, N], F32, name="ga_a%d" % t) for t in range(PACK)]
+        weighted_a = [keep.tile([P, N], F32, name="weighted_a%d" % t) for t in range(PACK)]
+        for t in range(PACK):
+            nc.scalar.activation(weighted_a[t][:], first[t][:], ACT.Copy, scale=ga_sb[:, t : t + 1])
 
         def fetch_members(c, t, gather):
-            mb = members.tile([P, N], F32, name="mb", bufs=16)
-            gather(mb[:], ex[t][:].indirect(entries(n1_sb, c * N, N)))
+            mb = keep.tile([P, P, MEMBERS], F32, name="mb%d_%d" % (c, t))
+            gather(mb[:].rearrange("p j u -> p (j u)"), ex[t][:].indirect(entries(n1_sb, c * P * MEMBERS, P * MEMBERS)))
             return mb
 
-        def sum_members(c, fetched, bank):
-            total = bank[:].rearrange("p (t j) -> p t j", t=PACK)
+        def sum_members(c, fetched):
+            total = first[c][:].rearrange("j (t p) -> j t p", t=PACK)
             for t in range(PACK):
-                mb = fetched[t] if t in fetched else fetch_members(c, t, scalar_gather)
-                addends = [ex[t][:, c * P : (c + 1) * P]] + [mb[:, u:N:4] for u in range(4)]
+                mb = fetched[t] if t in fetched else fetch_members(c, t, scalar_copy)
+                addends = [ex[t][:, c * P : (c + 1) * P]] + [mb[:, :, u] for u in range(MEMBERS)]
                 for u, addend in enumerate(addends):
                     nc.tensor.matmul(
-                        total[:, t, :], addend, identity[:], start=(u == 0), stop=(u == 4), is_transpose=True
+                        total[:, t, :], addend, identity[:], start=(u == 0), stop=(u == MEMBERS), is_transpose=True
                     )
-            return total
 
-        def weigh_a(t):
-            nc.scalar.activation(weighted_a[t][:], a_banks[t][:], ACT.Copy, scale=ga_sb[:, t : t + 1])
-
-        def logarithm(c, total):
+        def logarithm(c):
             log_turned = ring.tile([P, PACK, P], F32, name="log_turned")
-            nc.scalar.activation(log_turned[:], total, ACT.Ln)
-            log_bank = banks[c][:].rearrange("p (t j) -> p t j", t=PACK)
+            nc.scalar.activation(log_turned[:].rearrange("j t p -> j (t p)"), first[c][:], ACT.Ln)
             for t in range(PACK):
-                nc.tensor.transpose(log_bank[:, t, :], log_turned[:, t, :], identity[:])
-            return log_bank
+                nc.tensor.transpose(second[c][:, t * P : (t + 1) * P], log_turned[:, t, :], identity[:])
 
         def quantise_planes(planes, width, name):
             grouped = keep.tile([P, width, PACK], BF16, align_bytes=64, name=name + "_grouped")
@@ -207,75 +211,70 @@ def tile_picked_hkqglsekindggpair_none_p_kernel(
             )
             return words, scales
 
-        def finish_z(c, log_bank):
+        def quantise_z(c):
             z = ring.tile([P, PACK, P], F32, name="z")
             for t in range(PACK):
                 nc.vector.scalar_tensor_tensor(
                     z[:, t, :],
-                    log_bank[:, t, :],
+                    second[c][:, t * P : (t + 1) * P],
                     ga_sb[:, t : t + 1],
                     weighted_a[t][:, c * P : (c + 1) * P],
                     ALU.mult,
                     ALU.subtract,
                 )
-            return quantise_planes(z, P, "zblock%d" % c)
+            return quantise_planes(z, P, "z_block%d" % c)
 
         z2 = keep.tile([P, PACK, N], F32)
 
         def make_z2(t):
             kind = ring.tile([P, N], F32, name="kind")
-            for first in (0, 256):
-                part = slice(first, first + 256)
-                nc.vector.tensor_tensor(
-                    kind[:, part], tab_sb[t][:].indirect(entries(n2_sb, first, 256)), less_half[t][:, part], ALU.mult
-                )
-            for first in (0, 256):
-                part = slice(first, first + 256)
-                nc.vector.tensor_tensor(
-                    z2[:, t, part], less_half[t][:].indirect(entries(n3_sb, first, 256)), kind[:, part], ALU.subtract
-                )
-
-        def product_s(c, z_c, z2_q, bank, on_vector):
-            s_bank = product(bank, z_c[0][:], z_c[1][:], z2_q[0][:], z2_q[1][:])
-            if on_vector:
-                nc.vector.tensor_scalar(s_sb[c][:, :N], s_bank[:], 0.0625, None, ALU.mult)
-            else:
-                nc.scalar.activation(s_sb[c][:, :N], s_bank[:], ACT.Copy, scale=0.0625)
+            halves = [slice(h * HALF, (h + 1) * HALF) for h in range(2)]
+            for part in halves:
+                looked_up = twice_tab[t][:].indirect(entries(n2_sb, part.start, HALF))
+                nc.vector.tensor_tensor(kind[:, part], looked_up, less_half[t][:, part], ALU.mult)
+            for part in halves:
+                looked_up = less_half[t][:].indirect(entries(n3_sb, part.start, HALF))
+                nc.vector.tensor_tensor(z2[:, t, part], looked_up, kind[:, part], ALU.subtract)
 
         def fetch_pairs(c, h, gather):
-            pairs = members.tile([P, N // 2, 2], F32, name="pairs")
+            pairs = keep.tile([P, HALF, 2], F32, name="pairs%d_%d" % (c, h))
             gather(pairs[:].rearrange("p v u -> p (v u)"), s_sb[c][:].indirect(entries(n4_sb, h * N, N)))
             return pairs
 
         def finish_out(c, h, pairs):
-            part = slice(h * 256, (h + 1) * 256)
-            gap = ring.tile([P, N // 2], F32, name="gap")
+            part = slice(h * HALF, (h + 1) * HALF)
+            gap = ring.tile([P, HALF], F32, name="gap")
             nc.vector.tensor_tensor(gap[:], pairs[:, :, 0], s_sb[c][:, part], ALU.subtract)
-            lower = ring.tile([P, N // 2], F32, name="lower")
+            lower = ring.tile([P, HALF], F32, name="lower")
             nc.vector.scalar_tensor_tensor(lower[:], gap[:], 0.0, pairs[:, :, 1], ALU.min, ALU.add)
-            result = members.tile([P, N // 2], F32, name="result")
+            result = keep.tile([P, HALF], F32, name="result%d_%d" % (c, h))
             nc.vector.tensor_tensor(result[:], lower[:], pairs[:, :, 0], ALU.min)
             nc.sync.dma_start(out[c * P : (c + 1) * P, part], result[:])
 
-        early = {t: fetch_members(2, t, vector_gather) for t in range(2)}
-        totals = [sum_members(0, {}, banks[6]), sum_members(1, {}, banks[7])]
+        vector_share = {t: fetch_members(2, t, vector_copy) for t in range(PLANES_ON_VECTOR)}
+        sum_members(0, {})
+        sum_members(1, {})
         for t in range(PACK):
             make_z2(t)
-        for t in range(PACK):
-            weigh_a(t)
-        logs = [logarithm(0, totals[0])]
-        totals.append(sum_members(2, early, banks[4]))
-        logs.append(logarithm(1, totals[1]))
-        totals.append(sum_members(3, {}, banks[5]))
-        logs.append(logarithm(2, totals[2]))
-        logs.append(logarithm(3, totals[3]))
-        z2_q = quantise_planes(z2, N, "z2")
-        pairs = {}
-        for c in range(4):
-            product_s(c, finish_z(c, logs[c]), z2_q, banks[(6, 7, 4, 5)[c]], c in (0,))
+        logarithm(0)
+        sum_members(2, vector_share)
+        logarithm(1)
+        sum_members(3, {})
+        logarithm(2)
+        logarithm(3)
+        z2_words, z2_scales = quantise_planes(z2, N, "z2")
+
+        for c in range(BLOCKS):
+            z_words, z_scales = quantise_z(c)
+            product(first[c], z_words[:], z_scales[:], z2_words[:], z2_scales[:])
+            if c == BLOCKS - 1:
+                nc.vector.tensor_scalar(s_sb[c][:, :N], first[c][:], 0.0625, None, ALU.mult)
+            else:
+                nc.scalar.activation(s_sb[c][:, :N], first[c][:], ACT.Copy, scale=0.0625)
+            if c == 0:
+                first_pairs = fetch_pairs(0, 0, vector_copy)
+        finish_out(0, 0, first_pairs)
+        for c in range(BLOCKS):
             for h in range(2):
-                if (c, h) in ((0,0),):
-                    pairs[c, h] = fetch_pairs(c, h, vector_gather)
-        for c in range(4):
-            for h in range(2):
-                finish_out(c, h, pairs[c, h] if (c, h) in pairs else fetch_pairs(c, h, scalar_gather))
+                if (c, h) != (0, 0):
+                    finish_out(c, h, fetch_pairs(c, h, scalar_copy))

from contextlib import ExitStack

import concourse.mybir as mybir
from concourse.masks import make_identity

F32 = mybir.dt.float32
BF16 = mybir.dt.bfloat16
I32 = mybir.dt.int32
U32 = mybir.dt.uint32
U16 = mybir.dt.uint16
U8 = mybir.dt.uint8
FP8X4 = mybir.dt.float8_e4m3fn_x4
ALU = mybir.AluOpType
ACT = mybir.ActivationFunctionType

P = 128
PACK = 4
TOKENS = 2048
N = 512
HALF = N // 2
BLOCKS = N // P
MEMBERS = 4
GROUP = 16
QUADRANT = 32
SPARE = 32
W1_ON_SCALAR = 40
W2_ON_SCALAR = 32
PLANES_ON_VECTOR = 3
FLOPS = 3 * 2 * 512 * 512 * 512


def entries(lists, start, count):
    return lists[:, start // GROUP : (start + count) // GROUP]


def tile_picked_hkqglsekindggpair_none_p_kernel(
    tc, x_words, x_scales, w1, w2, tab, ga, gb, offs, two, n1, n2, n3, n4, out
):
    nc = tc.nc
    with ExitStack() as ctx:
        keep = ctx.enter_context(tc.tile_pool(name="keep", bufs=1))
        ring = ctx.enter_context(tc.tile_pool(name="ring", bufs=2))
        psum = ctx.enter_context(tc.psum_pool(name="psum", bufs=1))
        first = [psum.tile([P, N], F32, name="first%d" % i) for i in range(PACK)]
        second = [psum.tile([P, N], F32, name="second%d" % i) for i in range(PACK)]

        def scalar_copy(dst, src):
            nc.scalar.activation(dst, src, ACT.Copy)

        vector_copy = nc.vector.tensor_copy

        def load_list(lists, name):
            held = keep.tile(list(lists.shape), U16, name=name)
            nc.sync.dma_start(held[:], lists)
            return held

        def load_factor(factor, name):
            held = keep.tile([P, PACK], F32, name=name)
            nc.sync.dma_start(held[:], factor.rearrange("(p t) o -> p (t o)", t=PACK))
            return held

        def dealt(raw):
            return raw[:].rearrange("p j (m t) -> p m t j", t=PACK)

        def gathered_row(j):
            return slice(GROUP * (j // 2) + j, P, QUADRANT)

        byte_table = keep.tile([P, TOKENS], U8, align_bytes=64)
        nc.gpsimd.memset(byte_table[:].bitcast(I32), 0)
        offs_sb = load_list(offs, "offs_sb")
        w1_raw = keep.tile([P, PACK, N], F32)
        w1_rows = w1.rearrange("(p j) c -> p j c", j=PACK)
        nc.sync.dma_start(w1_raw[:, :1, :], w1_rows[:, :1, :])
        two_sb = load_list(two, "two_sb")
        for j in range(4):
            nc.sync.dma_start(byte_table[:].bitcast(I32)[gathered_row(j), :], x_scales[0].bitcast(I32)[j:16:4, :])
        word_table = keep.tile([P, TOKENS], I32, align_bytes=64)
        nc.sync.dma_start(word_table[:], x_words[0].rearrange("p n r -> p (n r)").bitcast(I32))
        nc.sync.dma_start(w1_raw[:, 1:, :], w1_rows[:, 1:, :])

        identity = keep.tile([P, P], F32)
        make_identity(nc, identity[:])
        ex = [keep.tile([P, N + SPARE], F32, name="ex%d" % t) for t in range(PACK)]
        s_sb = [keep.tile([P, N + SPARE], F32, name="s%d" % c) for c in range(BLOCKS)]
        for window in ex + s_sb:
            nc.gpsimd.memset(window[:, N:], 0.0)

        def pick_scales(lists, name):
            picked = keep.tile([P, N], U8, align_bytes=64, name=name + "_bytes")
            nc.vector.tensor_copy(picked[:], byte_table[:].indirect(lists[:]))
            scales = keep.tile([P, N], U8, align_bytes=64, name=name + "_scales")
            nc.vector.tensor_copy(scales[:].bitcast(I32), picked[:].bitcast(I32))
            for j in (2, 3):
                nc.sync.dma_start(scales[:].bitcast(I32)[j:P:QUADRANT, :], picked[:].bitcast(I32)[gathered_row(j), :])
            return scales

        def pick_words(lists, tag):
            picked = keep.tile([P, N], U32, align_bytes=64, name="picked_words", tag=tag)
            nc.vector.tensor_copy(picked[:], word_table[:].bitcast(U32).indirect(lists[:]))
            return picked

        def quantise_weight(name, shares):
            grouped = keep.tile([P, PACK, P, PACK], BF16, align_bytes=64, name=name + "_grouped")
            m = 0
            for copy_share, raw in shares:
                count = raw.shape[1]
                copy_share(grouped[:, :, m : m + count, :].rearrange("p t m j -> p m t j"), raw)
                m = m + count
            words = keep.tile([P, PACK, P], U32, align_bytes=64, name=name + "_words")
            scales = keep.tile([P, PACK, P], U8, align_bytes=64, name=name + "_scales")
            for t in range(PACK):
                nc.vector.quantize_mx(
                    out=words[:, t, :].bitcast(FP8X4),
                    scales=scales[:, t, :],
                    in_=grouped[:, t, :, :].rearrange("p m j -> p (m j)"),
                )
            return words, scales

        def product(bank, l_words, l_scales, r_words, r_scales):
            nc.tensor.matmul_mx(
                out=bank[:],
                lhsT=l_words.bitcast(FP8X4),
                lhsT_scale=l_scales,
                rhs=r_words.bitcast(FP8X4),
                rhs_scale=r_scales,
                start=True,
                stop=True,
            )

        def load_w2_half(h):
            raw = keep.tile([P, PACK, HALF], F32, name="w2_raw%d" % h)
            nc.sync.dma_start(raw[:], w2.rearrange("(p j) c -> p j c", j=PACK)[:, :, h * HALF : (h + 1) * HALF])
            return dealt(raw)

        w2_low = load_w2_half(0)
        xa_scales = pick_scales(offs_sb, "xa")
        xb_scales = pick_scales(two_sb, "xb")
        xa_words = pick_words(offs_sb, "xa_words")
        w1_words, w1_scales = quantise_weight(
            "w1",
            ((scalar_copy, dealt(w1_raw)[:, :W1_ON_SCALAR, :, :]), (vector_copy, dealt(w1_raw)[:, W1_ON_SCALAR:, :, :])),
        )
        xb_words = pick_words(two_sb, "w1_grouped")

        w2_high = load_w2_half(1)
        n1_sb = load_list(n1, "n1_sb")
        ga_sb = load_factor(ga, "ga_sb")
        gb_sb = load_factor(gb, "gb_sb")
        twice_tab = [keep.tile([P, N], F32, name="twice_tab%d" % t) for t in range(PACK)]
        for h in range(2):
            tab_raw = keep.tile([P, 2, N], F32, name="tab_raw%d" % h)
            nc.sync.dma_start(tab_raw[:], tab.rearrange("(p t) c -> p t c", t=PACK)[:, 2 * h : 2 * h + 2, :])
            for u in range(2):
                nc.gpsimd.tensor_scalar(twice_tab[2 * h + u][:], tab_raw[:, u, :], 2.0, 0.0, ALU.mult, ALU.add)
        n2_sb = load_list(n2, "n2_sb")
        n3_sb = load_list(n3, "n3_sb")
        n4_sb = load_list(n4, "n4_sb")

        for t in range(PACK):
            product(first[t], w1_words[:, t, :], w1_scales[:, t, :], xa_words[:], xa_scales[:])
            nc.scalar.activation(ex[t][:, :N], first[t][:], ACT.Exp)

        w2_words, w2_scales = quantise_weight(
            "w2",
            (
                (scalar_copy, w2_low[:, :W2_ON_SCALAR, :, :]),
                (vector_copy, w2_low[:, W2_ON_SCALAR:, :, :]),
                (vector_copy, w2_high),
            ),
        )
        less_half = [keep.tile([P, N], F32, name="less_half%d" % t) for t in range(PACK)]
        for t in range(PACK):
            product(second[t], w2_words[:, t, :], w2_scales[:, t, :], xb_words[:], xb_scales[:])
            nc.vector.tensor_scalar(less_half[t][:], second[t][:], gb_sb[:, t : t + 1], -0.5, ALU.mult, ALU.mult)

        weighted_a = [keep.tile([P, N], F32, name="weighted_a%d" % t) for t in range(PACK)]
        for t in range(PACK):
            nc.scalar.activation(weighted_a[t][:], first[t][:], ACT.Copy, scale=ga_sb[:, t : t + 1])

        def fetch_members(c, t, gather):
            mb = keep.tile([P, P, MEMBERS], F32, name="mb%d_%d" % (c, t))
            gather(mb[:].rearrange("p j u -> p (j u)"), ex[t][:].indirect(entries(n1_sb, c * P * MEMBERS, P * MEMBERS)))
            return mb

        def sum_members(c, fetched):
            total = first[c][:].rearrange("j (t p) -> j t p", t=PACK)
            for t in range(PACK):
                mb = fetched[t] if t in fetched else fetch_members(c, t, scalar_copy)
                addends = [ex[t][:, c * P : (c + 1) * P]] + [mb[:, :, u] for u in range(MEMBERS)]
                for u, addend in enumerate(addends):
                    nc.tensor.matmul(
                        total[:, t, :], addend, identity[:], start=(u == 0), stop=(u == MEMBERS), is_transpose=True
                    )

        def logarithm(c):
            log_turned = ring.tile([P, PACK, P], F32, name="log_turned")
            nc.scalar.activation(log_turned[:].rearrange("j t p -> j (t p)"), first[c][:], ACT.Ln)
            for t in range(PACK):
                nc.tensor.transpose(second[c][:, t * P : (t + 1) * P], log_turned[:, t, :], identity[:])

        def quantise_planes(planes, width, name):
            grouped = keep.tile([P, width, PACK], BF16, align_bytes=64, name=name + "_grouped")
            nc.vector.tensor_copy(
                grouped[:].rearrange("p (c i) t -> p c t i", i=4),
                planes[:].rearrange("p t (c i) -> p c t i", i=4),
            )
            words = keep.tile([P, width], U32, align_bytes=64, name=name + "_words")
            scales = keep.tile([P, width], U8, align_bytes=64, name=name + "_scales")
            nc.vector.quantize_mx(
                out=words[:].bitcast(FP8X4), scales=scales[:], in_=grouped[:].rearrange("p c t -> p (c t)")
            )
            return words, scales

        def quantise_z(c):
            z = ring.tile([P, PACK, P], F32, name="z")
            for t in range(PACK):
                nc.vector.scalar_tensor_tensor(
                    z[:, t, :],
                    second[c][:, t * P : (t + 1) * P],
                    ga_sb[:, t : t + 1],
                    weighted_a[t][:, c * P : (c + 1) * P],
                    ALU.mult,
                    ALU.subtract,
                )
            return quantise_planes(z, P, "z_block%d" % c)

        z2 = keep.tile([P, PACK, N], F32)

        def make_z2(t):
            kind = ring.tile([P, N], F32, name="kind")
            halves = [slice(h * HALF, (h + 1) * HALF) for h in range(2)]
            for part in halves:
                looked_up = twice_tab[t][:].indirect(entries(n2_sb, part.start, HALF))
                nc.vector.tensor_tensor(kind[:, part], looked_up, less_half[t][:, part], ALU.mult)
            for part in halves:
                looked_up = less_half[t][:].indirect(entries(n3_sb, part.start, HALF))
                nc.vector.tensor_tensor(z2[:, t, part], looked_up, kind[:, part], ALU.subtract)

        def fetch_pairs(c, h, gather):
            pairs = keep.tile([P, HALF, 2], F32, name="pairs%d_%d" % (c, h))
            gather(pairs[:].rearrange("p v u -> p (v u)"), s_sb[c][:].indirect(entries(n4_sb, h * N, N)))
            return pairs

        def finish_out(c, h, pairs):
            part = slice(h * HALF, (h + 1) * HALF)
            gap = ring.tile([P, HALF], F32, name="gap")
            nc.vector.tensor_tensor(gap[:], pairs[:, :, 0], s_sb[c][:, part], ALU.subtract)
            lower = ring.tile([P, HALF], F32, name="lower")
            nc.vector.scalar_tensor_tensor(lower[:], gap[:], 0.0, pairs[:, :, 1], ALU.min, ALU.add)
            result = keep.tile([P, HALF], F32, name="result%d_%d" % (c, h))
            nc.vector.tensor_tensor(result[:], lower[:], pairs[:, :, 0], ALU.min)
            nc.sync.dma_start(out[c * P : (c + 1) * P, part], result[:])

        vector_share = {t: fetch_members(2, t, vector_copy) for t in range(PLANES_ON_VECTOR)}
        sum_members(0, {})
        sum_members(1, {})
        for t in range(PACK):
            make_z2(t)
        logarithm(0)
        sum_members(2, vector_share)
        logarithm(1)
        sum_members(3, {})
        logarithm(2)
        logarithm(3)
        z2_words, z2_scales = quantise_planes(z2, N, "z2")

        for c in range(BLOCKS):
            z_words, z_scales = quantise_z(c)
            product(first[c], z_words[:], z_scales[:], z2_words[:], z2_scales[:])
            if c == BLOCKS - 1:
                nc.vector.tensor_scalar(s_sb[c][:, :N], first[c][:], 0.0625, None, ALU.mult)
            else:
                nc.scalar.activation(s_sb[c][:, :N], first[c][:], ACT.Copy, scale=0.0625)
            if c == 0:
                first_pairs = fetch_pairs(0, 0, vector_copy)
        finish_out(0, 0, first_pairs)
        for c in range(BLOCKS):
            for h in range(2):
                if (c, h) != (0, 0):
                    finish_out(c, h, fetch_pairs(c, h, scalar_copy))
